import numpy as np
import ml_dtypes


def mxq(x, axis, fmt="e4m3"):
    dtype, down = {"e4m3": (ml_dtypes.float8_e4m3fn, 7), "e5m2": (ml_dtypes.float8_e5m2, 14)}[fmt]
    v = np.moveaxis(np.asarray(x, np.float32).astype(ml_dtypes.bfloat16).astype(np.float64), axis, -1)
    blocks = v.reshape(v.shape[:-1] + (-1, 32))
    amax = np.abs(blocks).max(-1, keepdims=True)
    byte = np.maximum(np.where(amax > 0, np.frexp(amax)[1] - 1 + 127, 0) - down, 1)
    scale = np.exp2(byte - 127.0)
    codes = (blocks / scale).astype(np.float32).astype(dtype).astype(np.float64)
    return np.moveaxis((codes * scale).reshape(v.shape), -1, axis)


WIDE = False


def mx_kscale(k):
    if not WIDE:
        return np.ones(k)
    levels = np.array([30, -30])
    if k % 512:
        return np.exp2(np.random.permutation(np.resize(levels, k // 32))).repeat(32)
    a = np.empty((k // 512, 16))
    for p in range(k // 512):
        a[p, :8] = np.random.permutation(np.resize(levels, 8))
        for g in range(8):
            far = levels[np.abs(levels - a[p, g]) >= 10]
            a[p, g + 8] = far[np.random.randint(len(far))]
    return np.exp2(a.ravel()).repeat(32)


def f64(x):
    return np.asarray(x).astype(np.float64)


def striped(idx):
    return np.tile(np.asarray(idx).reshape(-1, 16).T, (8, 1)).astype(np.uint16)


def unstriped(offs):
    return offs[:16].T.reshape(-1).astype(np.int64)


E2M1 = np.array([0.0, 0.5, 1.0, 1.5, 2.0, 3.0, 4.0, 6.0, -0.0, -0.5, -1.0, -1.5, -2.0, -3.0, -4.0, -6.0])


def pack_weight(w, fmt):
    k, n = w.shape
    w = f64(np.asarray(w, np.float32).astype(ml_dtypes.bfloat16)).reshape(k // 32, 32, n)
    amax = np.abs(w).max(1)
    if fmt in ("e4m3", "e5m2"):
        byte = np.frexp(amax)[1] - 1 + 127 - (7 if fmt == "e4m3" else 14)
    else:
        mant, ex = np.frexp(amax / 6.0)
        byte = np.where(mant > 0.5, ex, ex - 1) + 127
    byte = np.clip(np.where(amax > 0, byte, 1), 1, 254)
    scaled = (w * np.exp2(127.0 - byte)[:, None, :]).reshape(k, n).astype(np.float32)
    by_word = np.ascontiguousarray(scaled.reshape(k // 512, 128, 4, n).transpose(0, 1, 3, 2))
    if fmt in ("e4m3", "e5m2"):
        words = by_word.astype(ml_dtypes.float8_e4m3fn if fmt == "e4m3" else ml_dtypes.float8_e5m2).view(np.uint8)
    else:
        c = by_word.astype(ml_dtypes.float4_e2m1fn).view(np.uint8) & 0xF
        words = (c[..., 0::2] | (c[..., 1::2] << 4)).reshape(k // 512, 128, 2 * n)
    return np.ascontiguousarray(words), np.ascontiguousarray(byte.astype(np.uint8).reshape(k // 512, 16, n))


def unpack_weight(words, scales, fmt):
    g, _, n = scales.shape
    words = np.ascontiguousarray(words).reshape(g, 128, n, -1)
    if fmt in ("e4m3", "e5m2"):
        vals = words.view(ml_dtypes.float8_e4m3fn if fmt == "e4m3" else ml_dtypes.float8_e5m2).astype(np.float64)
    else:
        nib = np.empty((g, 128, n, 4), np.uint8)
        nib[..., 0::2] = words & 0xF
        nib[..., 1::2] = words >> 4
        vals = E2M1[nib]
    vals = vals * np.repeat(np.exp2(scales.astype(np.float64) - 127.0), 8, axis=1)[..., None]
    return vals.transpose(0, 1, 3, 2).reshape(g * 512, n)


K, T, J, R, O, N = 512, 512, 256, 512, 128, 256


def setup_inputs():
    n = np.random.standard_normal
    idx = np.random.permutation(T)[:J]
    idx2 = np.random.permutation(J)[:O]
    idx3 = np.random.permutation(J)[:O]
    fk = mx_kscale(K)
    fr = mx_kscale(R)
    xtp = pack_weight(n((K, T)) / fk[:, None], "e2m1")
    wp = pack_weight(n((K, R)) * 1 / np.sqrt(K) * fk[:, None] * fr, "e5m2")
    wbp = pack_weight(n((R, N)) * 1 / np.sqrt(R) / fr[:, None], "e4m3")
    return {
        "xt_words": xtp[0],
        "xt_scales": xtp[1],
        "w_words": wp[0],
        "w_scales": wp[1],
        "wb_words": wbp[0],
        "wb_scales": wbp[1],
        "rs": (1.0 * n((O, N))).astype(np.float32),
        "offs": striped(idx),
        "offs2": striped(idx2),
        "offs3": striped(idx3),
    }


def reference(xt_words, xt_scales, w_words, w_scales, wb_words, wb_scales, rs, offs, offs2, offs3):
    idx = unstriped(offs)
    idx2 = unstriped(offs2)
    idx3 = unstriped(offs3)
    xtu = unpack_weight(xt_words, xt_scales, "e2m1")
    wu = unpack_weight(w_words, w_scales, "e5m2")
    wbu = unpack_weight(wb_words, wb_scales, "e4m3")
    xtidxg = xtu[:, idx]
    a = wu.T @ xtidxg
    ha = np.maximum(a, 0.0)
    hid = ha[:, idx2] - ha[:, idx3]
    hidq = mxq(hid, 0, "e5m2")
    p = hidq.T @ wbu
    pk2 = np.max(np.abs(p), axis=1, keepdims=True)
    y = p / (pk2 + 0.2) + 0.3 * f64(rs)
    return y

@@ -1,0 +1,144 @@
+from contextlib import ExitStack
+
+import concourse.mybir as mybir
+
+K, T, J, R, O, N = 512, 512, 256, 512, 128, 256
+FLOPS = 2 * K * R * J + 2 * R * O * N
+
+P = 128
+PACK = 4
+BANK = 512
+
+F32 = mybir.dt.float32
+BF16 = mybir.dt.bfloat16
+I32 = mybir.dt.int32
+U32 = mybir.dt.uint32
+U16 = mybir.dt.uint16
+U8 = mybir.dt.uint8
+E2M1X4 = mybir.dt.float4_e2m1fn_x4
+E5M2X4 = mybir.dt.float8_e5m2_x4
+E4M3X4 = mybir.dt.float8_e4m3fn_x4
+ALU = mybir.AluOpType
+ACT = mybir.ActivationFunctionType
+
+
+def load_scale_rows(queue, plane, scales, q):
+    rows = scales[0, 4 * q : 4 * q + 4, :].bitcast(I32)
+    queue.dma_start(
+        out=plane[32 * q : 32 * q + 32, :].bitcast(I32),
+        in_=rows.unsqueeze(0).to_broadcast([8, 4, rows.shape[1]]),
+    )
+
+
+def tile_list_looks_picked_gap_rowpeaks_kernel(
+    tc, xt_words, xt_scales, w_words, w_scales, wb_words, wb_scales, rs, offs, offs2, offs3, out
+):
+    nc = tc.nc
+    with ExitStack() as ctx:
+        sb = ctx.enter_context(tc.tile_pool(name="sb", bufs=1))
+        ps = ctx.enter_context(tc.psum_pool(name="ps", bufs=1))
+
+        def tile(name, shape, dtype):
+            return sb.tile(shape, dtype, name=name, align_bytes=64)
+
+        idx = tile("idx", [P, J // 16], U16)
+        idx2 = tile("idx2", [P, O // 16], U16)
+        idx3 = tile("idx3", [P, O // 16], U16)
+        xw = tile("xw", [P, T], U16)
+        xs = tile("xs", [P, T], U8)
+        ww = tile("ww", [P, R], U32)
+        ws = tile("ws", [P, R], U8)
+        wbw = tile("wbw", [P, N], U32)
+        wbs = tile("wbs", [P, N], U8)
+        res = tile("res", [P, N], F32)
+
+        nc.sync.dma_start(idx[:], offs)
+        nc.scalar.dma_start(out=xw[:].bitcast(I32), in_=xt_words[0].bitcast(I32))
+        load_scale_rows(nc.sync, xs, xt_scales, 0)
+        load_scale_rows(nc.scalar, xs, xt_scales, 1)
+        load_scale_rows(nc.sync, xs, xt_scales, 2)
+        load_scale_rows(nc.scalar, xs, xt_scales, 3)
+        load_scale_rows(nc.sync, ws, w_scales, 0)
+        nc.scalar.dma_start(out=ww[:].bitcast(I32), in_=w_words[0].rearrange("p c t -> p (c t)").bitcast(I32))
+        for q in range(1, 4):
+            load_scale_rows(nc.sync, ws, w_scales, q)
+        nc.sync.dma_start(idx2[:], offs2)
+        nc.sync.dma_start(idx3[:], offs3)
+        nc.sync.dma_start(out=res[:], in_=rs)
+        nc.sync.dma_start(out=wbw[:].bitcast(I32), in_=wb_words[0].rearrange("p c t -> p (c t)").bitcast(I32))
+        for q in range(4):
+            load_scale_rows(nc.sync, wbs, wb_scales, q)
+
+        xgw = tile("xgw", [P, J], U16)
+        xgs = tile("xgs", [P, J], U8)
+        nc.vector.tensor_copy(xgw[:], xw[:].indirect(idx[:]))
+        nc.vector.tensor_copy(xgs[:], xs[:].indirect(idx[:]))
+
+        wpw = tile("wpw", [P, R], U32)
+        wps = tile("wps", [P, R], U8)
+        nc.vector.tensor_copy(
+            wpw[:].rearrange("p (t m) -> p m t", t=PACK), ww[:].rearrange("p (m t) -> p m t", t=PACK)
+        )
+        nc.vector.tensor_copy(
+            wps[:].rearrange("p (t m) -> p m t", t=PACK), ws[:].rearrange("p (m t) -> p m t", t=PACK)
+        )
+
+        res3 = tile("res3", [P, N], F32)
+        nc.scalar.activation(res3[:], res[:], ACT.Copy, scale=0.3)
+
+        g2 = tile("g2", [P, PACK, O], F32)
+        g3 = tile("g3", [P, PACK, O], F32)
+        ha = []
+        for t in range(PACK):
+            cols = slice(t * P, (t + 1) * P)
+            a = ps.tile([P, BANK], F32, name="a%d" % t)
+            nc.tensor.matmul_mx(
+                out=a[:, :J],
+                lhsT=wpw[:, cols].bitcast(E5M2X4),
+                lhsT_scale=wps[:, cols],
+                rhs=xgw[:].bitcast(E2M1X4),
+                rhs_scale=xgs[:],
+                start=True,
+                stop=True,
+            )
+            h = tile("ha%d" % t, [P, J], F32)
+            if t % 2 == 0:
+                nc.scalar.activation(h[:], a[:, :J], ACT.Relu)
+            else:
+                nc.vector.tensor_scalar(h[:], a[:, :J], 0.0, None, ALU.max)
+            ha.append(h)
+        for t in range(PACK):
+            nc.vector.tensor_copy(g2[:, t, :], ha[t][:].indirect(idx2[:]))
+            nc.scalar.activation(g3[:, t, :], ha[t][:].indirect(idx3[:]), ACT.Copy)
+
+        hid = tile("hid", [P, O * PACK], BF16)
+        nc.vector.tensor_tensor(
+            hid[:].rearrange("p (c i t) -> p c t i", i=4, t=PACK),
+            g2[:].rearrange("p t (c i) -> p c t i", i=4),
+            g3[:].rearrange("p t (c i) -> p c t i", i=4),
+            ALU.subtract,
+        )
+        hw = tile("hw", [P, O], U32)
+        hs = tile("hs", [P, O], U8)
+        nc.vector.quantize_mx(out=hw[:].bitcast(E5M2X4), scales=hs[:], in_=hid[:])
+
+        pp = ps.tile([P, BANK], F32, name="pp")
+        nc.tensor.matmul_mx(
+            out=pp[:, :N],
+            lhsT=hw[:].bitcast(E5M2X4),
+            lhsT_scale=hs[:],
+            rhs=wbw[:].bitcast(E4M3X4),
+            rhs_scale=wbs[:],
+            start=True,
+            stop=True,
+        )
+        mag = tile("mag", [P, N], F32)
+        nc.scalar.activation(mag[:], pp[:, :N], ACT.Abs)
+        shifted = tile("shifted", [P, N], F32)
+        den = tile("den", [P, 1], F32)
+        nc.vector.tensor_scalar(shifted[:], mag[:], 0.2, None, ALU.add, ALU.max, accum_out=den[:])
+        inv = tile("inv", [P, 1], F32)
+        nc.vector.reciprocal(inv[:], den[:])
+        y = tile("y", [P, N], F32)
+        nc.vector.scalar_tensor_tensor(y[:], pp[:, :N], inv[:], res3[:], ALU.mult, ALU.add)
+        nc.sync.dma_start(out=out, in_=y[:])

@@ -30,6 +30,22 @@ def load_scale_rows(queue, plane, scales, q):
     )
 
 
+def load_scale_upper(queue, plane, scales):
+    rows = scales[0, 2:16, :].bitcast(I32)
+    queue.dma_start(
+        out=plane[16:128, :].bitcast(I32),
+        in_=rows.unsqueeze(0).to_broadcast([8, 14, rows.shape[1]]),
+    )
+
+
+def load_scale_lower(queue, plane, scales):
+    rows = scales[0, 0:4, :].bitcast(I32)
+    queue.dma_start(
+        out=plane[0:16, :].bitcast(I32),
+        in_=rows.unsqueeze(0).to_broadcast([4, 4, rows.shape[1]]),
+    )
+
+
 def tile_list_looks_picked_gap_rowpeaks_kernel(
     tc, xt_words, xt_scales, w_words, w_scales, wb_words, wb_scales, rs, offs, offs2, offs3, out
 ):
@@ -54,20 +70,17 @@ def tile_list_looks_picked_gap_rowpeaks_kernel(
 
         nc.sync.dma_start(idx[:], offs)
         nc.scalar.dma_start(out=xw[:].bitcast(I32), in_=xt_words[0].bitcast(I32))
-        load_scale_rows(nc.sync, xs, xt_scales, 0)
-        load_scale_rows(nc.scalar, xs, xt_scales, 1)
-        load_scale_rows(nc.sync, xs, xt_scales, 2)
-        load_scale_rows(nc.scalar, xs, xt_scales, 3)
-        load_scale_rows(nc.sync, ws, w_scales, 0)
+        load_scale_lower(nc.sync, xs, xt_scales)
         nc.scalar.dma_start(out=ww[:].bitcast(I32), in_=w_words[0].rearrange("p c t -> p (c t)").bitcast(I32))
-        for q in range(1, 4):
-            load_scale_rows(nc.sync, ws, w_scales, q)
-        nc.sync.dma_start(idx2[:], offs2)
+        load_scale_upper(nc.sync, xs, xt_scales)
+        load_scale_upper(nc.scalar, ws, w_scales)
+        load_scale_lower(nc.sync, ws, w_scales)
         nc.sync.dma_start(idx3[:], offs3)
-        nc.sync.dma_start(out=res[:], in_=rs)
+        nc.sync.dma_start(idx2[:], offs2)
         nc.sync.dma_start(out=wbw[:].bitcast(I32), in_=wb_words[0].rearrange("p c t -> p (c t)").bitcast(I32))
         for q in range(4):
             load_scale_rows(nc.sync, wbs, wb_scales, q)
+        nc.sync.dma_start(out=res[:], in_=rs)
 
         xgw = tile("xgw", [P, J], U16)
         xgs = tile("xgs", [P, J], U8)
@@ -76,15 +89,13 @@ def tile_list_looks_picked_gap_rowpeaks_kernel(
 
         wpw = tile("wpw", [P, R], U32)
         wps = tile("wps", [P, R], U8)
-        nc.vector.tensor_copy(
-            wpw[:].rearrange("p (t m) -> p m t", t=PACK), ww[:].rearrange("p (m t) -> p m t", t=PACK)
-        )
-        nc.vector.tensor_copy(
-            wps[:].rearrange("p (t m) -> p m t", t=PACK), ws[:].rearrange("p (m t) -> p m t", t=PACK)
-        )
-
-        res3 = tile("res3", [P, N], F32)
-        nc.scalar.activation(res3[:], res[:], ACT.Copy, scale=0.3)
+        for u in range(2):
+            pair = slice(2 * u, 2 * u + 2)
+            for dealt, loaded in ((wpw, ww), (wps, ws)):
+                nc.vector.tensor_copy(
+                    dealt[:].rearrange("p (t m) -> p m t", t=PACK)[:, :, pair],
+                    loaded[:].rearrange("p (m t) -> p m t", t=PACK)[:, :, pair],
+                )
 
         g2 = tile("g2", [P, PACK, O], F32)
         g3 = tile("g3", [P, PACK, O], F32)
@@ -110,6 +121,9 @@ def tile_list_looks_picked_gap_rowpeaks_kernel(
         for t in range(PACK):
             nc.vector.tensor_copy(g2[:, t, :], ha[t][:].indirect(idx2[:]))
             nc.scalar.activation(g3[:, t, :], ha[t][:].indirect(idx3[:]), ACT.Copy)
+
+        res3 = tile("ha3", [P, N], F32)
+        nc.scalar.activation(res3[:], res[:], ACT.Copy, scale=0.3)
 
         hid = tile("hid", [P, O * PACK], BF16)
         nc.vector.tensor_tensor(

@@ -68,13 +68,13 @@ def tile_list_looks_picked_gap_rowpeaks_kernel(
         wbs = tile("wbs", [P, N], U8)
         res = tile("res", [P, N], F32)
 
+        nc.sync.dma_start(out=xw[:].bitcast(I32), in_=xt_words[0].bitcast(I32))
+        load_scale_upper(nc.scalar, xs, xt_scales)
         nc.sync.dma_start(idx[:], offs)
-        nc.scalar.dma_start(out=xw[:].bitcast(I32), in_=xt_words[0].bitcast(I32))
         load_scale_lower(nc.sync, xs, xt_scales)
-        nc.scalar.dma_start(out=ww[:].bitcast(I32), in_=w_words[0].rearrange("p c t -> p (c t)").bitcast(I32))
-        load_scale_upper(nc.sync, xs, xt_scales)
-        load_scale_upper(nc.scalar, ws, w_scales)
+        nc.sync.dma_start(out=ww[:].bitcast(I32), in_=w_words[0].rearrange("p c t -> p (c t)").bitcast(I32))
         load_scale_lower(nc.sync, ws, w_scales)
+        load_scale_upper(nc.scalar, ws, w_scales)
         nc.sync.dma_start(idx3[:], offs3)
         nc.sync.dma_start(idx2[:], offs2)
         nc.sync.dma_start(out=wbw[:].bitcast(I32), in_=wb_words[0].rearrange("p c t -> p (c t)").bitcast(I32))
@@ -87,54 +87,64 @@ def tile_list_looks_picked_gap_rowpeaks_kernel(
         nc.vector.tensor_copy(xgw[:], xw[:].indirect(idx[:]))
         nc.vector.tensor_copy(xgs[:], xs[:].indirect(idx[:]))
 
-        wpw = tile("wpw", [P, R], U32)
-        wps = tile("wps", [P, R], U8)
-        for u in range(2):
-            pair = slice(2 * u, 2 * u + 2)
-            for dealt, loaded in ((wpw, ww), (wps, ws)):
-                nc.vector.tensor_copy(
-                    dealt[:].rearrange("p (t m) -> p m t", t=PACK)[:, :, pair],
-                    loaded[:].rearrange("p (m t) -> p m t", t=PACK)[:, :, pair],
-                )
+        wpw = [tile("wpw0", [P, 2 * P], U32), tile("ws", [P, 2 * P], U32)]
+        wps = [tile("wps%d" % u, [P, 2 * P], U8) for u in range(2)]
+        for dealt, loaded, u in ((wpw, ww, 0), (wps, ws, 0), (wps, ws, 1), (wpw, ww, 1)):
+            nc.vector.tensor_copy(
+                dealt[u][:].rearrange("p (t m) -> p m t", t=2),
+                loaded[:].rearrange("p (m t) -> p m t", t=PACK)[:, :, 2 * u : 2 * u + 2],
+            )
 
         g2 = tile("g2", [P, PACK, O], F32)
         g3 = tile("g3", [P, PACK, O], F32)
         ha = []
         for t in range(PACK):
-            cols = slice(t * P, (t + 1) * P)
+            cols = slice((t % 2) * P, (t % 2 + 1) * P)
             a = ps.tile([P, BANK], F32, name="a%d" % t)
             nc.tensor.matmul_mx(
                 out=a[:, :J],
-                lhsT=wpw[:, cols].bitcast(E5M2X4),
-                lhsT_scale=wps[:, cols],
+                lhsT=wpw[t // 2][:, cols].bitcast(E5M2X4),
+                lhsT_scale=wps[t // 2][:, cols],
                 rhs=xgw[:].bitcast(E2M1X4),
                 rhs_scale=xgs[:],
                 start=True,
                 stop=True,
             )
             h = tile("ha%d" % t, [P, J], F32)
-            if t % 2 == 0:
+            if t != 1:
                 nc.scalar.activation(h[:], a[:, :J], ACT.Relu)
             else:
                 nc.vector.tensor_scalar(h[:], a[:, :J], 0.0, None, ALU.max)
             ha.append(h)
-        for t in range(PACK):
-            nc.vector.tensor_copy(g2[:, t, :], ha[t][:].indirect(idx2[:]))
-            nc.scalar.activation(g3[:, t, :], ha[t][:].indirect(idx3[:]), ACT.Copy)
+        for picked, lst, on_vector in ((g3, idx3, (0, 1)), (g2, idx2, (0, 1, 2))):
+            for t in range(PACK):
+                if t in on_vector:
+                    nc.vector.tensor_copy(picked[:, t, :], ha[t][:].indirect(lst[:]))
+                else:
+                    nc.scalar.activation(picked[:, t, :], ha[t][:].indirect(lst[:]), ACT.Copy)
 
         res3 = tile("ha3", [P, N], F32)
         nc.scalar.activation(res3[:], res[:], ACT.Copy, scale=0.3)
 
         hid = tile("hid", [P, O * PACK], BF16)
-        nc.vector.tensor_tensor(
-            hid[:].rearrange("p (c i t) -> p c t i", i=4, t=PACK),
-            g2[:].rearrange("p t (c i) -> p c t i", i=4),
-            g3[:].rearrange("p t (c i) -> p c t i", i=4),
-            ALU.subtract,
-        )
         hw = tile("hw", [P, O], U32)
         hs = tile("hs", [P, O], U8)
-        nc.vector.quantize_mx(out=hw[:].bitcast(E5M2X4), scales=hs[:], in_=hid[:])
+        half = O // 2
+        for u in range(2):
+            places = slice(u * half, (u + 1) * half)
+            nc.vector.tensor_tensor(
+                hid[:, u * half * PACK : (u + 1) * half * PACK].rearrange("p (c i t) -> p c t i", i=4, t=PACK),
+                g2[:, :, places].rearrange("p t (c i) -> p c t i", i=4),
+                g3[:, :, places].rearrange("p t (c i) -> p c t i", i=4),
+                ALU.subtract,
+            )
+        for u in range(2):
+            places = slice(u * half, (u + 1) * half)
+            nc.vector.quantize_mx(
+                out=hw[:, places].bitcast(E5M2X4),
+                scales=hs[:, places],
+                in_=hid[:, u * half * PACK : (u + 1) * half * PACK],
+            )
 
         pp = ps.tile([P, BANK], F32, name="pp")
         nc.tensor.matmul_mx(

@@ -89,11 +89,17 @@ def tile_list_looks_picked_gap_rowpeaks_kernel(
 
         wpw = [tile("wpw0", [P, 2 * P], U32), tile("ws", [P, 2 * P], U32)]
         wps = [tile("wps%d" % u, [P, 2 * P], U8) for u in range(2)]
-        for dealt, loaded, u in ((wpw, ww, 0), (wps, ws, 0), (wps, ws, 1), (wpw, ww, 1)):
+
+        def deal(dealt, loaded, u, walk):
             nc.vector.tensor_copy(
-                dealt[u][:].rearrange("p (t m) -> p m t", t=2),
-                loaded[:].rearrange("p (m t) -> p m t", t=PACK)[:, :, 2 * u : 2 * u + 2],
+                dealt[u][:].rearrange("p (t m) -> " + walk, t=2),
+                loaded[:].rearrange("p (m t) -> p m t", t=PACK)[:, :, 2 * u : 2 * u + 2].rearrange("p m t -> " + walk),
             )
+
+        deal(wpw, ww, 0, "p m t")
+        deal(wps, ws, 0, "p t m")
+        deal(wps, ws, 1, "p t m")
+        deal(wpw, ww, 1, "p m t")
 
         g2 = tile("g2", [P, PACK, O], F32)
         g3 = tile("g3", [P, PACK, O], F32)
@@ -146,23 +152,30 @@ def tile_list_looks_picked_gap_rowpeaks_kernel(
                 in_=hid[:, u * half * PACK : (u + 1) * half * PACK],
             )
 
-        pp = ps.tile([P, BANK], F32, name="pp")
-        nc.tensor.matmul_mx(
-            out=pp[:, :N],
-            lhsT=hw[:].bitcast(E5M2X4),
-            lhsT_scale=hs[:],
-            rhs=wbw[:].bitcast(E4M3X4),
-            rhs_scale=wbs[:],
-            start=True,
-            stop=True,
-        )
+        hn = N // 2
         mag = tile("mag", [P, N], F32)
-        nc.scalar.activation(mag[:], pp[:, :N], ACT.Abs)
+        pp = []
+        for u in range(2):
+            cols = slice(u * hn, (u + 1) * hn)
+            bank = ps.tile([P, BANK], F32, name="pp%d" % u)
+            nc.tensor.matmul_mx(
+                out=bank[:, :hn],
+                lhsT=hw[:].bitcast(E5M2X4),
+                lhsT_scale=hs[:],
+                rhs=wbw[:, cols].bitcast(E4M3X4),
+                rhs_scale=wbs[:, cols],
+                start=True,
+                stop=True,
+            )
+            nc.scalar.activation(mag[:, cols], bank[:, :hn], ACT.Abs)
+            pp.append(bank)
         shifted = tile("shifted", [P, N], F32)
         den = tile("den", [P, 1], F32)
         nc.vector.tensor_scalar(shifted[:], mag[:], 0.2, None, ALU.add, ALU.max, accum_out=den[:])
         inv = tile("inv", [P, 1], F32)
         nc.vector.reciprocal(inv[:], den[:])
         y = tile("y", [P, N], F32)
-        nc.vector.scalar_tensor_tensor(y[:], pp[:, :N], inv[:], res3[:], ALU.mult, ALU.add)
+        for u in range(2):
+            cols = slice(u * hn, (u + 1) * hn)
+            nc.vector.scalar_tensor_tensor(y[:, cols], pp[u][:, :hn], inv[:], res3[:, cols], ALU.mult, ALU.add)
         nc.sync.dma_start(out=out, in_=y[:])

from contextlib import ExitStack

import concourse.mybir as mybir

K, T, J, R, O, N = 512, 512, 256, 512, 128, 256
FLOPS = 2 * K * R * J + 2 * R * O * N

P = 128
PACK = 4
BANK = 512

F32 = mybir.dt.float32
BF16 = mybir.dt.bfloat16
I32 = mybir.dt.int32
U32 = mybir.dt.uint32
U16 = mybir.dt.uint16
U8 = mybir.dt.uint8
E2M1X4 = mybir.dt.float4_e2m1fn_x4
E5M2X4 = mybir.dt.float8_e5m2_x4
E4M3X4 = mybir.dt.float8_e4m3fn_x4
ALU = mybir.AluOpType
ACT = mybir.ActivationFunctionType


def load_scale_rows(queue, plane, scales, q):
    rows = scales[0, 4 * q : 4 * q + 4, :].bitcast(I32)
    queue.dma_start(
        out=plane[32 * q : 32 * q + 32, :].bitcast(I32),
        in_=rows.unsqueeze(0).to_broadcast([8, 4, rows.shape[1]]),
    )


def load_scale_upper(queue, plane, scales):
    rows = scales[0, 2:16, :].bitcast(I32)
    queue.dma_start(
        out=plane[16:128, :].bitcast(I32),
        in_=rows.unsqueeze(0).to_broadcast([8, 14, rows.shape[1]]),
    )


def load_scale_lower(queue, plane, scales):
    rows = scales[0, 0:4, :].bitcast(I32)
    queue.dma_start(
        out=plane[0:16, :].bitcast(I32),
        in_=rows.unsqueeze(0).to_broadcast([4, 4, rows.shape[1]]),
    )


def tile_list_looks_picked_gap_rowpeaks_kernel(
    tc, xt_words, xt_scales, w_words, w_scales, wb_words, wb_scales, rs, offs, offs2, offs3, out
):
    nc = tc.nc
    with ExitStack() as ctx:
        sb = ctx.enter_context(tc.tile_pool(name="sb", bufs=1))
        ps = ctx.enter_context(tc.psum_pool(name="ps", bufs=1))

        def tile(name, shape, dtype):
            return sb.tile(shape, dtype, name=name, align_bytes=64)

        idx = tile("idx", [P, J // 16], U16)
        idx2 = tile("idx2", [P, O // 16], U16)
        idx3 = tile("idx3", [P, O // 16], U16)
        xw = tile("xw", [P, T], U16)
        xs = tile("xs", [P, T], U8)
        ww = tile("ww", [P, R], U32)
        ws = tile("ws", [P, R], U8)
        wbw = tile("wbw", [P, N], U32)
        wbs = tile("wbs", [P, N], U8)
        res = tile("res", [P, N], F32)

        nc.sync.dma_start(out=xw[:].bitcast(I32), in_=xt_words[0].bitcast(I32))
        load_scale_upper(nc.scalar, xs, xt_scales)
        nc.sync.dma_start(idx[:], offs)
        load_scale_lower(nc.sync, xs, xt_scales)
        nc.sync.dma_start(out=ww[:].bitcast(I32), in_=w_words[0].rearrange("p c t -> p (c t)").bitcast(I32))
        load_scale_lower(nc.sync, ws, w_scales)
        load_scale_upper(nc.scalar, ws, w_scales)
        nc.sync.dma_start(idx3[:], offs3)
        nc.sync.dma_start(idx2[:], offs2)
        nc.sync.dma_start(out=wbw[:].bitcast(I32), in_=wb_words[0].rearrange("p c t -> p (c t)").bitcast(I32))
        for q in range(4):
            load_scale_rows(nc.sync, wbs, wb_scales, q)
        nc.sync.dma_start(out=res[:], in_=rs)

        xgw = tile("xgw", [P, J], U16)
        xgs = tile("xgs", [P, J], U8)
        nc.vector.tensor_copy(xgw[:], xw[:].indirect(idx[:]))
        nc.vector.tensor_copy(xgs[:], xs[:].indirect(idx[:]))

        wpw = [tile("wpw0", [P, 2 * P], U32), tile("ws", [P, 2 * P], U32)]
        wps = [tile("wps%d" % u, [P, 2 * P], U8) for u in range(2)]

        def deal(dealt, loaded, u, walk):
            nc.vector.tensor_copy(
                dealt[u][:].rearrange("p (t m) -> " + walk, t=2),
                loaded[:].rearrange("p (m t) -> p m t", t=PACK)[:, :, 2 * u : 2 * u + 2].rearrange("p m t -> " + walk),
            )

        deal(wpw, ww, 0, "p m t")
        deal(wps, ws, 0, "p t m")
        deal(wps, ws, 1, "p t m")
        deal(wpw, ww, 1, "p m t")

        g2 = tile("g2", [P, PACK, O], F32)
        g3 = tile("g3", [P, PACK, O], F32)
        ha = []
        for t in range(PACK):
            cols = slice((t % 2) * P, (t % 2 + 1) * P)
            a = ps.tile([P, BANK], F32, name="a%d" % t)
            nc.tensor.matmul_mx(
                out=a[:, :J],
                lhsT=wpw[t // 2][:, cols].bitcast(E5M2X4),
                lhsT_scale=wps[t // 2][:, cols],
                rhs=xgw[:].bitcast(E2M1X4),
                rhs_scale=xgs[:],
                start=True,
                stop=True,
            )
            h = tile("ha%d" % t, [P, J], F32)
            if t != 1:
                nc.scalar.activation(h[:], a[:, :J], ACT.Relu)
            else:
                nc.vector.tensor_scalar(h[:], a[:, :J], 0.0, None, ALU.max)
            ha.append(h)
        for picked, lst, on_vector in ((g3, idx3, (0, 1)), (g2, idx2, (0, 1, 2))):
            for t in range(PACK):
                if t in on_vector:
                    nc.vector.tensor_copy(picked[:, t, :], ha[t][:].indirect(lst[:]))
                else:
                    nc.scalar.activation(picked[:, t, :], ha[t][:].indirect(lst[:]), ACT.Copy)

        res3 = tile("ha3", [P, N], F32)
        nc.scalar.activation(res3[:], res[:], ACT.Copy, scale=0.3)

        hid = tile("hid", [P, O * PACK], BF16)
        hw = tile("hw", [P, O], U32)
        hs = tile("hs", [P, O], U8)
        half = O // 2
        for u in range(2):
            places = slice(u * half, (u + 1) * half)
            nc.vector.tensor_tensor(
                hid[:, u * half * PACK : (u + 1) * half * PACK].rearrange("p (c i t) -> p c t i", i=4, t=PACK),
                g2[:, :, places].rearrange("p t (c i) -> p c t i", i=4),
                g3[:, :, places].rearrange("p t (c i) -> p c t i", i=4),
                ALU.subtract,
            )
        for u in range(2):
            places = slice(u * half, (u + 1) * half)
            nc.vector.quantize_mx(
                out=hw[:, places].bitcast(E5M2X4),
                scales=hs[:, places],
                in_=hid[:, u * half * PACK : (u + 1) * half * PACK],
            )

        hn = N // 2
        mag = tile("mag", [P, N], F32)
        pp = []
        for u in range(2):
            cols = slice(u * hn, (u + 1) * hn)
            bank = ps.tile([P, BANK], F32, name="pp%d" % u)
            nc.tensor.matmul_mx(
                out=bank[:, :hn],
                lhsT=hw[:].bitcast(E5M2X4),
                lhsT_scale=hs[:],
                rhs=wbw[:, cols].bitcast(E4M3X4),
                rhs_scale=wbs[:, cols],
                start=True,
                stop=True,
            )
            nc.scalar.activation(mag[:, cols], bank[:, :hn], ACT.Abs)
            pp.append(bank)
        shifted = tile("shifted", [P, N], F32)
        den = tile("den", [P, 1], F32)
        nc.vector.tensor_scalar(shifted[:], mag[:], 0.2, None, ALU.add, ALU.max, accum_out=den[:])
        inv = tile("inv", [P, 1], F32)
        nc.vector.reciprocal(inv[:], den[:])
        y = tile("y", [P, N], F32)
        for u in range(2):
            cols = slice(u * hn, (u + 1) * hn)
            nc.vector.scalar_tensor_tensor(y[:, cols], pp[u][:, :hn], inv[:], res3[:, cols], ALU.mult, ALU.add)
        nc.sync.dma_start(out=out, in_=y[:])
